import numpy as np
import ml_dtypes


def mxq(x, axis, fmt="e4m3"):
    dtype, down = {"e4m3": (ml_dtypes.float8_e4m3fn, 7), "e5m2": (ml_dtypes.float8_e5m2, 14)}[fmt]
    v = np.moveaxis(np.asarray(x, np.float32).astype(ml_dtypes.bfloat16).astype(np.float64), axis, -1)
    blocks = v.reshape(v.shape[:-1] + (-1, 32))
    amax = np.abs(blocks).max(-1, keepdims=True)
    byte = np.maximum(np.where(amax > 0, np.frexp(amax)[1] - 1 + 127, 0) - down, 1)
    scale = np.exp2(byte - 127.0)
    codes = (blocks / scale).astype(np.float32).astype(dtype).astype(np.float64)
    return np.moveaxis((codes * scale).reshape(v.shape), -1, axis)


WIDE = False


def mx_kscale(k):
    if not WIDE:
        return np.ones(k)
    levels = np.array([10, -10, 5, -5, 0])
    if k % 512:
        return np.exp2(np.random.permutation(np.resize(levels, k // 32))).repeat(32)
    a = np.empty((k // 512, 16))
    for p in range(k // 512):
        a[p, :8] = np.random.permutation(np.resize(levels, 8))
        for g in range(8):
            far = levels[np.abs(levels - a[p, g]) >= 10]
            a[p, g + 8] = far[np.random.randint(len(far))]
    return np.exp2(a.ravel()).repeat(32)


def f64(x):
    return np.asarray(x).astype(np.float64)


def striped(idx):
    return np.tile(idx.reshape(-1, 16).T, (8, 1)).astype(np.uint16)


def unstriped(offs):
    return offs[:16].T.reshape(-1).astype(np.int64)


def striped8(idx):
    return np.concatenate([x.reshape(-1, 16).T for x in idx]).astype(np.uint16)


def runs(offs, k):
    lists = np.stack([offs[16 * r : 16 * r + 16].T.reshape(-1) for r in range(8)]).astype(np.int64)
    return lists[np.arange(k) % 512 // 64]


def pack_weight(w):
    k, n = w.shape
    w = f64(np.asarray(w, np.float32).astype(ml_dtypes.bfloat16)).reshape(k // 32, 32, n)
    amax = np.abs(w).max(1)
    byte = np.clip(np.where(amax > 0, np.frexp(amax)[1] - 1 + 127 - 7, 1), 1, 254)
    scaled = (w * np.exp2(127.0 - byte)[:, None, :]).reshape(k, n).astype(np.float32)
    words = np.ascontiguousarray(scaled.reshape(k // 512, 128, 4, n).transpose(0, 1, 3, 2)).astype(ml_dtypes.float8_e4m3fn).view(np.uint8)
    return words, np.ascontiguousarray(byte.astype(np.uint8).reshape(k // 512, 16, n))


def unpack_weight(words, scales):
    g, p, n, _ = words.shape
    vals = np.ascontiguousarray(words).view(ml_dtypes.float8_e4m3fn).astype(np.float64) * np.repeat(np.exp2(scales.astype(np.float64) - 127.0), 8, axis=1)[..., None]
    return vals.transpose(0, 1, 3, 2).reshape(g * 512, n)


def relu(v):
    return np.maximum(v, 0.0)


K, T, S, N, H = 512, 2048, 512, 512, 512


def setup_inputs():
    n = np.random.standard_normal
    s = mx_kscale(K)[:, None]
    u = mx_kscale(H)
    packed_xT = pack_weight(n((K, T)) * s)
    return {
        "x_words": packed_xT[0],
        "x_scales": packed_xT[1],
        "w1": (n((K, H)) / np.sqrt(K) / s).astype(np.float32),
        "gn": (np.random.uniform(0.5, 1.5, (H, 1)) * u[:, None]).astype(np.float32),
        "gm": (np.random.uniform(0.5, 1.5, (H, 1)) * u[:, None]).astype(np.float32),
        "w2": (n((H, N)) / np.sqrt(2 * H) / u[:, None]).astype(np.float32),
        "w3": (n((H, N)) / np.sqrt(2 * H) / u[:, None]).astype(np.float32),
        "offs": striped(np.random.permutation(T)[:S]),
        "n1": striped8(np.stack([np.random.permutation(S) for _ in range(8)])),
        "n2": striped8(np.stack([np.random.permutation(S) for _ in range(8)])),
        "n3": striped8(np.stack([np.random.permutation(S) for _ in range(8)])),
        "n4": striped8(np.stack([np.random.permutation(S) for _ in range(8)])),
        "n5": striped8(np.stack([np.random.permutation(S) for _ in range(8)])),
        "n6": striped8(np.stack([np.random.permutation(S) for _ in range(8)])),
    }


def reference(x_words, x_scales, w1, gn, gm, w2, w3, offs, n1, n2, n3, n4, n5, n6):
    xq = unpack_weight(x_words, x_scales)[:, unstriped(offs)]
    y = mxq(f64(w1), 0, "e4m3").T @ xq
    z = f64(gn) * (np.minimum(np.maximum(y, y[np.arange(H)[:, None], runs(n1, H)]), y[np.arange(H)[:, None], runs(n2, H)]))
    z2 = f64(gm) * (relu(y - (y[np.arange(H)[:, None], runs(n3, H)])) + 0.5 * (relu(y[np.arange(H)[:, None], runs(n4, H)] - y)))
    h = mxq(f64(w2), 0, "e4m3").T @ mxq(z, 0, "e4m3") + mxq(f64(w3), 0, "e4m3").T @ mxq(z2, 0, "e4m3")
    return 0.75 * (h[np.arange(N)[:, None], runs(n5, N)] + h[np.arange(N)[:, None], runs(n6, N)]) - h

@@ -1,0 +1,191 @@
+from contextlib import ExitStack
+
+import concourse.mybir as mybir
+
+K, T, S, H, N = 512, 2048, 512, 512, 512
+FLOPS = 2 * K * H * S + 2 * 2 * H * N * S
+
+F32 = mybir.dt.float32
+BF16 = mybir.dt.bfloat16
+I32 = mybir.dt.int32
+U32 = mybir.dt.uint32
+U16 = mybir.dt.uint16
+U8 = mybir.dt.uint8
+FP8X4 = mybir.dt.float8_e4m3fn_x4
+ALU = mybir.AluOpType
+ACT = mybir.ActivationFunctionType
+
+P = 128
+PACK = 4
+STRIPE = 16
+CHUNKS = [(0, 256), (256, 384), (384, 512)]
+
+
+def entries(offsets, lo, hi):
+    return offsets[:, lo // STRIPE : hi // STRIPE]
+
+
+def tile_picked_joinminmxhingelap_none_p_kernel(tc, x_words, x_scales, w1, gn, gm, w2, w3, offs, n1, n2, n3, n4, n5, n6, out):
+    nc = tc.nc
+    with ExitStack() as ctx:
+        keep = ctx.enter_context(tc.tile_pool(name="keep", bufs=1))
+        ring = ctx.enter_context(tc.tile_pool(name="ring", bufs=3))
+        psum = ctx.enter_context(tc.psum_pool(name="psum", bufs=1))
+
+        def load_list(src, name):
+            tile = keep.tile([P, S // STRIPE], U16, name=name)
+            nc.sync.dma_start(tile[:], src)
+            return tile
+
+        def load_weight(src, name):
+            tile = keep.tile([P, PACK * src.shape[1]], F32, name=name)
+            nc.sync.dma_start(tile[:], src.rearrange("(p j) c -> p (j c)", j=PACK))
+            return tile
+
+        def load_gain(src, name):
+            tile = keep.tile([P, PACK], F32, name=name)
+            nc.sync.dma_start(tile[:], src.rearrange("(p t) o -> p (t o)", t=PACK))
+            return tile
+
+        def quantize(grouped, name):
+            width = grouped.shape[1] // PACK
+            codes = keep.tile([P, width], U32, name=name + "_codes", align_bytes=64)
+            scales = keep.tile([P, width], U8, name=name + "_scales", align_bytes=64)
+            nc.vector.quantize_mx(out=codes[:].bitcast(FP8X4), scales=scales[:], in_=grouped[:])
+            return codes, scales
+
+        def deal_weight(copy, raw, t0, t1, name):
+            grouped = keep.tile([P, (t1 - t0) * P * PACK], BF16, name=name, align_bytes=64)
+            copy(
+                grouped[:].rearrange("p (t m j) -> p m j t", m=P, j=PACK),
+                raw[:].rearrange("p (j m t) -> p m j t", j=PACK, t=PACK)[:, :, :, t0:t1],
+            )
+            return grouped
+
+        def interleave(planes, name):
+            width = planes.shape[1] // PACK
+            grouped = keep.tile([P, PACK * width], BF16, name=name, align_bytes=64)
+            nc.scalar.copy(
+                grouped[:].rearrange("p (c i t) -> p c t i", i=4, t=PACK),
+                planes[:].rearrange("p (t c i) -> p c t i", t=PACK, i=4),
+            )
+            return grouped
+
+        def product(acc, left, m0, right, lo, hi, start, stop):
+            nc.tensor.matmul_mx(
+                out=acc,
+                lhsT=left[0][:, m0 : m0 + P].bitcast(FP8X4),
+                lhsT_scale=left[1][:, m0 : m0 + P],
+                rhs=right[0][:, lo:hi].bitcast(FP8X4),
+                rhs_scale=right[1][:, lo:hi],
+                start=start,
+                stop=stop,
+            )
+
+        x_scale_table = keep.tile([P, T], U8, name="x_scale_table")
+        nc.vector.memset(x_scale_table[:].bitcast(I32), 0)
+        w1_raw = load_weight(w1, "w1_raw")
+        picks = load_list(offs, "picks")
+        for q in range(4):
+            nc.sync.dma_start(
+                x_scale_table[32 * q : 32 * q + 4, :].bitcast(I32),
+                x_scales[0, 4 * q : 4 * q + 4, :].bitcast(I32),
+            )
+        x_word_table = keep.tile([P, T], I32, name="x_word_table")
+        nc.sync.dma_start(x_word_table[:], x_words[0].rearrange("p c r -> p (c r)").bitcast(I32))
+        gm_tile = load_gain(gm, "gm_tile")
+        list1 = load_list(n1, "list1")
+        list2 = load_list(n2, "list2")
+        gn_tile = load_gain(gn, "gn_tile")
+        list3 = load_list(n3, "list3")
+        w2_raw = load_weight(w2, "w2_raw")
+        w3_raw = load_weight(w3, "w3_raw")
+        list4 = load_list(n4, "list4")
+        list5 = load_list(n5, "list5")
+        list6 = load_list(n6, "list6")
+
+        windows = [keep.tile([P, 2 * S], F32, name=f"window{t}") for t in range(PACK)]
+        for t in range(PACK):
+            nc.vector.memset(windows[t][:, S:], 0.0)
+
+        z2_gain = keep.tile([P, PACK], F32, name="z2_gain")
+        nc.scalar.activation(z2_gain[:], gm_tile[:], ACT.Copy, scale=-0.5)
+
+        x_codes = keep.tile([P, S], U32, name="x_codes", align_bytes=64)
+        x_bytes = keep.tile([P, S], U8, name="x_bytes", align_bytes=64)
+        nc.vector.tensor_copy(x_bytes[:], x_scale_table[:].indirect(picks[:]))
+        w1_low = deal_weight(nc.vector.tensor_copy, w1_raw, 0, 2, "w1_low")
+        w1_high = deal_weight(nc.scalar.copy, w1_raw, 2, 4, "w1_high")
+        w1_q = [quantize(w1_low, "w1_low"), quantize(w1_high, "w1_high")]
+        half = S // 2
+        for lo in (0, half):
+            nc.vector.tensor_copy(
+                x_codes[:, lo : lo + half], x_word_table[:].bitcast(U32).indirect(entries(picks, lo, lo + half))
+            )
+        x_q = (x_codes, x_bytes)
+
+        y_first = [psum.tile([P, half], F32, name=f"y_first{u}") for u in range(2)]
+        y_banks = [psum.tile([P, S], F32, name=f"bank{t}") for t in range(1, PACK)]
+        neg_y = [keep.tile([P, S], F32, name=f"neg_y{t}") for t in range(PACK)]
+        for u in range(2):
+            product(y_first[u][:], w1_q[0], 0, x_q, u * half, (u + 1) * half, True, True)
+            nc.scalar.copy(windows[0][:, u * half : (u + 1) * half], y_first[u][:])
+        for t in range(1, PACK):
+            product(y_banks[t - 1][:], w1_q[t // 2], (t % 2) * P, x_q, 0, S, True, True)
+            nc.scalar.copy(windows[t][:, :S], y_banks[t - 1][:])
+        for t in range(PACK):
+            nc.scalar.activation(neg_y[t][:], windows[t][:, :S], ACT.Copy, scale=-1.0)
+
+        z_planes = keep.tile([P, PACK * S], BF16, name="z_planes")
+        for t in range(PACK):
+            y1 = ring.tile([P, S], F32, name="y1")
+            y2 = ring.tile([P, S], F32, name="y2")
+            larger = ring.tile([P, S], F32, name="larger")
+            smaller = ring.tile([P, S], F32, name="smaller")
+            nc.vector.tensor_copy(y1[:], windows[t][:].indirect(list1[:]))
+            nc.vector.tensor_copy(y2[:], windows[t][:].indirect(list2[:]))
+            nc.vector.tensor_tensor(larger[:], windows[t][:, :S], y1[:], ALU.max)
+            nc.vector.tensor_tensor(smaller[:], larger[:], y2[:], ALU.min)
+            nc.scalar.activation(z_planes[:, t * S : (t + 1) * S], smaller[:], ACT.Copy, scale=gn_tile[:, t : t + 1])
+        z_grouped = interleave(z_planes, "z_grouped")
+
+        w2_grouped = deal_weight(nc.scalar.copy, w2_raw, 0, PACK, "w2_grouped")
+        w3_grouped = deal_weight(nc.scalar.copy, w3_raw, 0, PACK, "w3_grouped")
+
+        hinge3 = [keep.tile([P, S], F32, name=f"hinge3_{t}") for t in range(PACK)]
+        for t in range(PACK):
+            d3 = ring.tile([P, S], F32, name="d3")
+            nc.vector.tensor_tensor(d3[:], windows[t][:].indirect(list3[:]), neg_y[t][:], ALU.add)
+            nc.scalar.activation(hinge3[t][:], d3[:], ACT.Relu, scale=-2.0)
+        w2_q = quantize(w2_grouped, "w2")
+        w3_q = quantize(w3_grouped, "w3")
+        z_q = quantize(z_grouped, "z")
+
+        h_banks = [psum.tile([P, S], F32, name=f"bank{t}") for t in range(PACK)]
+        neg_h = [keep.tile([P, S], F32, name=f"neg_h{t}") for t in range(PACK)]
+        for lo, hi in CHUNKS:
+            width = hi - lo
+            z2_planes = keep.tile([P, PACK * width], BF16, name=f"z2_planes{lo}")
+            for t in range(PACK):
+                d4 = keep.tile([P, width], F32, name=f"d4_{lo}_{t}")
+                both = keep.tile([P, width], F32, name=f"both_{lo}_{t}")
+                nc.vector.tensor_tensor(d4[:], neg_y[t][:].indirect(entries(list4, lo, hi)), windows[t][:, lo:hi], ALU.add)
+                nc.vector.scalar_tensor_tensor(both[:], d4[:], 0.0, hinge3[t][:, lo:hi], ALU.min, ALU.subtract)
+                nc.scalar.activation(z2_planes[:, t * width : (t + 1) * width], both[:], ACT.Copy, scale=z2_gain[:, t : t + 1])
+            z2_q = quantize(interleave(z2_planes, f"z2_grouped{lo}"), f"z2_{lo}")
+            for t in range(PACK):
+                product(h_banks[t][:, lo:hi], w2_q, t * P, z_q, lo, hi, True, False)
+                product(h_banks[t][:, lo:hi], w3_q, t * P, z2_q, 0, width, False, True)
+                nc.scalar.activation(windows[t][:, lo:hi], h_banks[t][:, lo:hi], ACT.Copy, scale=0.75)
+                nc.scalar.activation(neg_h[t][:, lo:hi], h_banks[t][:, lo:hi], ACT.Copy, scale=-1.0)
+
+        out_rows = out.rearrange("(p t) n -> p t n", t=PACK)
+        partial = [keep.tile([P, S], F32, name=f"partial{t}") for t in range(PACK)]
+        for t in range(PACK):
+            nc.vector.tensor_tensor(partial[t][:], windows[t][:].indirect(list5[:]), neg_h[t][:], ALU.add)
+        for t in range(PACK):
+            pieces = [(0, S)] if t < PACK - 1 else [(0, half), (half, S)]
+            for lo, hi in pieces:
+                result = keep.tile([P, hi - lo], F32, name=f"result{t}_{lo}")
+                nc.vector.tensor_tensor(result[:], windows[t][:].indirect(entries(list6, lo, hi)), partial[t][:, lo:hi], ALU.add)
+                nc.sync.dma_start(out_rows[:, t, lo:hi], result[:])

@@ -1,6 +1,7 @@
 from contextlib import ExitStack
 
 import concourse.mybir as mybir
+from concourse.masks import make_identity
 
 K, T, S, H, N = 512, 2048, 512, 512, 512
 FLOPS = 2 * K * H * S + 2 * 2 * H * N * S
@@ -30,6 +31,7 @@ def tile_picked_joinminmxhingelap_none_p_kernel(tc, x_words, x_scales, w1, gn, g
     with ExitStack() as ctx:
         keep = ctx.enter_context(tc.tile_pool(name="keep", bufs=1))
         ring = ctx.enter_context(tc.tile_pool(name="ring", bufs=3))
+        trio = ctx.enter_context(tc.tile_pool(name="trio", bufs=3))
         psum = ctx.enter_context(tc.psum_pool(name="psum", bufs=1))
 
         def load_list(src, name):
@@ -47,12 +49,13 @@ def tile_picked_joinminmxhingelap_none_p_kernel(tc, x_words, x_scales, w1, gn, g
             nc.sync.dma_start(tile[:], src.rearrange("(p t) o -> p (t o)", t=PACK))
             return tile
 
-        def quantize(grouped, name):
-            width = grouped.shape[1] // PACK
+        def packed(width, name):
             codes = keep.tile([P, width], U32, name=name + "_codes", align_bytes=64)
             scales = keep.tile([P, width], U8, name=name + "_scales", align_bytes=64)
-            nc.vector.quantize_mx(out=codes[:].bitcast(FP8X4), scales=scales[:], in_=grouped[:])
             return codes, scales
+
+        def quantize(dest, lo, hi, grouped):
+            nc.vector.quantize_mx(out=dest[0][:, lo:hi].bitcast(FP8X4), scales=dest[1][:, lo:hi], in_=grouped)
 
         def deal_weight(copy, raw, t0, t1, name):
             grouped = keep.tile([P, (t1 - t0) * P * PACK], BF16, name=name, align_bytes=64)
@@ -64,7 +67,7 @@ def tile_picked_joinminmxhingelap_none_p_kernel(tc, x_words, x_scales, w1, gn, g
 
         def interleave(planes, name):
             width = planes.shape[1] // PACK
-            grouped = keep.tile([P, PACK * width], BF16, name=name, align_bytes=64)
+            grouped = keep.tile([P, PACK * width], BF16, name=name, tag=name, align_bytes=64)
             nc.scalar.copy(
                 grouped[:].rearrange("p (c i t) -> p c t i", i=4, t=PACK),
                 planes[:].rearrange("p (t c i) -> p c t i", t=PACK, i=4),
@@ -94,8 +97,8 @@ def tile_picked_joinminmxhingelap_none_p_kernel(tc, x_words, x_scales, w1, gn, g
         x_word_table = keep.tile([P, T], I32, name="x_word_table")
         nc.sync.dma_start(x_word_table[:], x_words[0].rearrange("p c r -> p (c r)").bitcast(I32))
         gm_tile = load_gain(gm, "gm_tile")
-        list1 = load_list(n1, "list1")
         list2 = load_list(n2, "list2")
+        list1 = load_list(n1, "list1")
         gn_tile = load_gain(gn, "gn_tile")
         list3 = load_list(n3, "list3")
         w2_raw = load_weight(w2, "w2_raw")
@@ -116,7 +119,9 @@ def tile_picked_joinminmxhingelap_none_p_kernel(tc, x_words, x_scales, w1, gn, g
         nc.vector.tensor_copy(x_bytes[:], x_scale_table[:].indirect(picks[:]))
         w1_low = deal_weight(nc.vector.tensor_copy, w1_raw, 0, 2, "w1_low")
         w1_high = deal_weight(nc.scalar.copy, w1_raw, 2, 4, "w1_high")
-        w1_q = [quantize(w1_low, "w1_low"), quantize(w1_high, "w1_high")]
+        w1_q = [packed(2 * P, "w1_low"), packed(2 * P, "w1_high")]
+        quantize(w1_q[0], 0, 2 * P, w1_low[:])
+        quantize(w1_q[1], 0, 2 * P, w1_high[:])
         half = S // 2
         for lo in (0, half):
             nc.vector.tensor_copy(
@@ -124,68 +129,120 @@ def tile_picked_joinminmxhingelap_none_p_kernel(tc, x_words, x_scales, w1, gn, g
             )
         x_q = (x_codes, x_bytes)
 
-        y_first = [psum.tile([P, half], F32, name=f"y_first{u}") for u in range(2)]
+        y_first = [psum.tile([P, half], F32, name=f"turn{u}") for u in range(2)]
         y_banks = [psum.tile([P, S], F32, name=f"bank{t}") for t in range(1, PACK)]
         neg_y = [keep.tile([P, S], F32, name=f"neg_y{t}") for t in range(PACK)]
         for u in range(2):
+            cols = slice(u * half, (u + 1) * half)
             product(y_first[u][:], w1_q[0], 0, x_q, u * half, (u + 1) * half, True, True)
-            nc.scalar.copy(windows[0][:, u * half : (u + 1) * half], y_first[u][:])
+            nc.scalar.copy(windows[0][:, cols], y_first[u][:])
+            nc.scalar.activation(neg_y[0][:, cols], y_first[u][:], ACT.Copy, scale=-1.0)
         for t in range(1, PACK):
             product(y_banks[t - 1][:], w1_q[t // 2], (t % 2) * P, x_q, 0, S, True, True)
             nc.scalar.copy(windows[t][:, :S], y_banks[t - 1][:])
-        for t in range(PACK):
-            nc.scalar.activation(neg_y[t][:], windows[t][:, :S], ACT.Copy, scale=-1.0)
-
-        z_planes = keep.tile([P, PACK * S], BF16, name="z_planes")
-        for t in range(PACK):
-            y1 = ring.tile([P, S], F32, name="y1")
-            y2 = ring.tile([P, S], F32, name="y2")
-            larger = ring.tile([P, S], F32, name="larger")
-            smaller = ring.tile([P, S], F32, name="smaller")
-            nc.vector.tensor_copy(y1[:], windows[t][:].indirect(list1[:]))
-            nc.vector.tensor_copy(y2[:], windows[t][:].indirect(list2[:]))
-            nc.vector.tensor_tensor(larger[:], windows[t][:, :S], y1[:], ALU.max)
-            nc.vector.tensor_tensor(smaller[:], larger[:], y2[:], ALU.min)
-            nc.scalar.activation(z_planes[:, t * S : (t + 1) * S], smaller[:], ACT.Copy, scale=gn_tile[:, t : t + 1])
-        z_grouped = interleave(z_planes, "z_grouped")
+            nc.scalar.activation(neg_y[t][:], y_banks[t - 1][:], ACT.Copy, scale=-1.0)
 
         w2_grouped = deal_weight(nc.scalar.copy, w2_raw, 0, PACK, "w2_grouped")
         w3_grouped = deal_weight(nc.scalar.copy, w3_raw, 0, PACK, "w3_grouped")
 
-        hinge3 = [keep.tile([P, S], F32, name=f"hinge3_{t}") for t in range(PACK)]
+        identity = keep.tile([P, P], F32, name="identity")
+        make_identity(nc, identity[:])
+        z_planes = keep.tile([P, PACK * S], BF16, name="z_planes")
+        d1_all = keep.tile([P, PACK * S], F32, name="wide_gap")
         for t in range(PACK):
-            d3 = ring.tile([P, S], F32, name="d3")
-            nc.vector.tensor_tensor(d3[:], windows[t][:].indirect(list3[:]), neg_y[t][:], ALU.add)
-            nc.scalar.activation(hinge3[t][:], d3[:], ACT.Relu, scale=-2.0)
-        w2_q = quantize(w2_grouped, "w2")
-        w3_q = quantize(w3_grouped, "w3")
-        z_q = quantize(z_grouped, "z")
+            d1 = d1_all[:, t * S : (t + 1) * S]
+            d2 = [trio.tile([P, half], F32, name="gap", align_bytes=64) for lo in (0, half)]
+            shift = keep.tile([P, S], F32, name=f"shift{t}")
+            nc.vector.tensor_tensor(d2[0][:], windows[t][:].indirect(entries(list2, 0, half)), neg_y[t][:, :half], ALU.add)
+            nc.vector.tensor_tensor(d1, windows[t][:].indirect(list1[:]), neg_y[t][:], ALU.add)
+            nc.vector.tensor_tensor(d2[1][:], windows[t][:].indirect(entries(list2, half, S)), neg_y[t][:, half:], ALU.add)
+            for lo in (0, half):
+                nc.vector.scalar_tensor_tensor(
+                    shift[:, lo : lo + half], d1[:, lo : lo + half], 0.0, d2[lo // half][:], ALU.max, ALU.min
+                )
+            turned = psum.tile([P, S], F32, name=f"turn{t % 2}")
+            for c in range(0, S, P):
+                nc.tensor.matmul(turned[:, c : c + P], windows[t][:, c : c + P], identity[:], start=True, stop=False, is_transpose=True)
+                nc.tensor.matmul(turned[:, c : c + P], shift[:, c : c + P], identity[:], start=False, stop=True, is_transpose=True)
+            turned_sum = ring.tile([P, S], F32, name="turned_sum")
+            nc.scalar.copy(turned_sum[:], turned[:])
+            back = psum.tile([P, S], F32, name=f"back{t % 2}")
+            for c in range(0, S, P):
+                nc.tensor.transpose(back[:, c : c + P], turned_sum[:, c : c + P], identity[:])
+            nc.scalar.activation(z_planes[:, t * S : (t + 1) * S], back[:], ACT.Copy, scale=gn_tile[:, t : t + 1])
+        z_grouped = interleave(z_planes, "z_grouped")
 
-        h_banks = [psum.tile([P, S], F32, name=f"bank{t}") for t in range(PACK)]
-        neg_h = [keep.tile([P, S], F32, name=f"neg_h{t}") for t in range(PACK)]
-        for lo, hi in CHUNKS:
+        hinge_all = keep.tile([P, PACK * S], F32, name="z_planes")
+        hinge3 = [hinge_all[:, t * S : (t + 1) * S] for t in range(PACK)]
+        d3_all = keep.tile([P, PACK * S], F32, name="wide_gap")
+        for t in range(PACK):
+            d3 = d3_all[:, t * S : (t + 1) * S]
+            nc.vector.tensor_tensor(d3, windows[t][:].indirect(list3[:]), neg_y[t][:], ALU.add)
+            nc.scalar.activation(hinge3[t], d3, ACT.Relu, scale=-2.0)
+        w2_first, w3_first = packed(P, "w2_first"), packed(P, "w3_first")
+        z_q, z2_q = packed(S, "z"), packed(S, "z2")
+        quantize(w2_first, 0, P, w2_grouped[:, : PACK * P])
+        quantize(w3_first, 0, P, w3_grouped[:, : PACK * P])
+        quantize(z_q, 0, S, z_grouped[:])
+
+        h_banks = [None] + [psum.tile([P, S], F32, name=f"bank{t}") for t in range(1, PACK)]
+        neg_h = [keep.tile([P, S], F32, name=f"neg_h{t}", tag=f"neg_h{t}") for t in range(PACK)]
+        steps = [(lo, hi, t) for lo, hi in CHUNKS for t in range(PACK)]
+        bank_tags = {0: "turn0", 256: "turn1", 384: "bank0"}
+        z2_planes = {lo: keep.tile([P, PACK * (hi - lo)], BF16, name=f"z2_planes{lo}") for lo, hi in CHUNKS}
+
+        def fetch_gap4(lo, hi, t):
+            d4 = trio.tile([P, hi - lo], F32, name="gap", align_bytes=64)
+            nc.vector.tensor_tensor(d4[:], neg_y[t][:].indirect(entries(list4, lo, hi)), windows[t][:, lo:hi], ALU.add)
+            return d4
+
+        def finish_step(d4, lo, hi, t):
             width = hi - lo
-            z2_planes = keep.tile([P, PACK * width], BF16, name=f"z2_planes{lo}")
-            for t in range(PACK):
-                d4 = keep.tile([P, width], F32, name=f"d4_{lo}_{t}")
-                both = keep.tile([P, width], F32, name=f"both_{lo}_{t}")
-                nc.vector.tensor_tensor(d4[:], neg_y[t][:].indirect(entries(list4, lo, hi)), windows[t][:, lo:hi], ALU.add)
-                nc.vector.scalar_tensor_tensor(both[:], d4[:], 0.0, hinge3[t][:, lo:hi], ALU.min, ALU.subtract)
-                nc.scalar.activation(z2_planes[:, t * width : (t + 1) * width], both[:], ACT.Copy, scale=z2_gain[:, t : t + 1])
-            z2_q = quantize(interleave(z2_planes, f"z2_grouped{lo}"), f"z2_{lo}")
-            for t in range(PACK):
-                product(h_banks[t][:, lo:hi], w2_q, t * P, z_q, lo, hi, True, False)
-                product(h_banks[t][:, lo:hi], w3_q, t * P, z2_q, 0, width, False, True)
-                nc.scalar.activation(windows[t][:, lo:hi], h_banks[t][:, lo:hi], ACT.Copy, scale=0.75)
-                nc.scalar.activation(neg_h[t][:, lo:hi], h_banks[t][:, lo:hi], ACT.Copy, scale=-1.0)
+            both_tag = "z2_grouped0" if (lo, t) == (CHUNKS[1][0], 2) else f"both_{lo}_{t}"
+            both = keep.tile([P, width], F32, name="both", tag=both_tag, align_bytes=64)
+            nc.vector.scalar_tensor_tensor(both[:], d4[:], 0.0, hinge3[t][:, lo:hi], ALU.min, ALU.subtract)
+            nc.scalar.activation(z2_planes[lo][:, t * width : (t + 1) * width], both[:], ACT.Copy, scale=z2_gain[:, t : t + 1])
+            if t == PACK - 1:
+                h_first = psum.tile([P, width], F32, name="h_first", tag=bank_tags[lo])
+                quantize(z2_q, lo, hi, interleave(z2_planes[lo], f"z2_grouped{lo}")[:])
+                product(h_first[:], w2_first, 0, z_q, lo, hi, True, False)
+                product(h_first[:], w3_first, 0, z2_q, lo, hi, False, True)
+                nc.scalar.activation(windows[0][:, lo:hi], h_first[:], ACT.Copy, scale=0.75)
+                nc.scalar.activation(neg_h[0][:, lo:hi], h_first[:], ACT.Copy, scale=-1.0)
+
+        fetched = fetch_gap4(*steps[0])
+        for k, step in enumerate(steps):
+            ahead = fetch_gap4(*steps[k + 1]) if k + 1 < len(steps) else None
+            finish_step(fetched, *step)
+            fetched = ahead
+
+        second_codes = trio.tile([P, 2 * P], U32, name="gap", align_bytes=64)
+        second_scales = keep.tile([P, 2 * P], U8, name="second_scales", align_bytes=64)
+        rest_codes = trio.tile([P, 4 * P], U32, name="gap", align_bytes=64)
+        rest_scales = keep.tile([P, 4 * P], U8, name="rest_scales", align_bytes=64)
+        second, rest = (second_codes, second_scales), (rest_codes, rest_scales)
+        quantize(second, 0, P, w2_grouped[:, PACK * P : 2 * PACK * P])
+        quantize(second, P, 2 * P, w3_grouped[:, PACK * P : 2 * PACK * P])
+        quantize(rest, 0, 2 * P, w2_grouped[:, 2 * PACK * P :])
+        quantize(rest, 2 * P, 4 * P, w3_grouped[:, 2 * PACK * P :])
+        for t in range(1, PACK):
+            left, m2, m3 = (second, 0, P) if t == 1 else (rest, (t - 2) * P, t * P)
+            product(h_banks[t][:], left, m2, z_q, 0, S, True, False)
+            product(h_banks[t][:], left, m3, z2_q, 0, S, False, True)
+            nc.scalar.activation(windows[t][:, :S], h_banks[t][:], ACT.Copy, scale=0.75)
+            nc.scalar.activation(neg_h[t][:], h_banks[t][:], ACT.Copy, scale=-1.0)
 
         out_rows = out.rearrange("(p t) n -> p t n", t=PACK)
-        partial = [keep.tile([P, S], F32, name=f"partial{t}") for t in range(PACK)]
         for t in range(PACK):
-            nc.vector.tensor_tensor(partial[t][:], windows[t][:].indirect(list5[:]), neg_h[t][:], ALU.add)
-        for t in range(PACK):
-            pieces = [(0, S)] if t < PACK - 1 else [(0, half), (half, S)]
-            for lo, hi in pieces:
-                result = keep.tile([P, hi - lo], F32, name=f"result{t}_{lo}")
-                nc.vector.tensor_tensor(result[:], windows[t][:].indirect(entries(list6, lo, hi)), partial[t][:, lo:hi], ALU.add)
-                nc.sync.dma_start(out_rows[:, t, lo:hi], result[:])
+            partial = keep.tile([P, S], F32, name=f"partial{t}")
+            result = keep.tile([P, S], F32, name=f"result{t}")
+            for lo in (0, half):
+                cols = slice(lo, lo + half)
+                nc.vector.tensor_tensor(partial[:, cols], windows[t][:].indirect(entries(list5, lo, lo + half)), neg_h[t][:, cols], ALU.add)
+            for lo in (0, half):
+                cols = slice(lo, lo + half)
+                nc.vector.tensor_tensor(result[:, cols], windows[t][:].indirect(entries(list6, lo, lo + half)), partial[:, cols], ALU.add)
+                if t == PACK - 1:
+                    nc.sync.dma_start(out_rows[:, t, cols], result[:, cols])
+            if t < PACK - 1:
+                nc.sync.dma_start(out_rows[:, t, :], result[:])

@@ -94,7 +94,7 @@ def tile_picked_joinminmxhingelap_none_p_kernel(tc, x_words, x_scales, w1, gn, g
                 x_scale_table[32 * q : 32 * q + 4, :].bitcast(I32),
                 x_scales[0, 4 * q : 4 * q + 4, :].bitcast(I32),
             )
-        x_word_table = keep.tile([P, T], I32, name="x_word_table")
+        x_word_table = keep.tile([P, T], I32, name="x_word_table", align_bytes=64)
         nc.sync.dma_start(x_word_table[:], x_words[0].rearrange("p c r -> p (c r)").bitcast(I32))
         gm_tile = load_gain(gm, "gm_tile")
         list2 = load_list(n2, "list2")
@@ -117,17 +117,20 @@ def tile_picked_joinminmxhingelap_none_p_kernel(tc, x_words, x_scales, w1, gn, g
         x_codes = keep.tile([P, S], U32, name="x_codes", align_bytes=64)
         x_bytes = keep.tile([P, S], U8, name="x_bytes", align_bytes=64)
         nc.vector.tensor_copy(x_bytes[:], x_scale_table[:].indirect(picks[:]))
-        w1_low = deal_weight(nc.vector.tensor_copy, w1_raw, 0, 2, "w1_low")
+        w1_low = deal_weight(nc.scalar.copy, w1_raw, 0, 2, "w1_low")
         w1_high = deal_weight(nc.scalar.copy, w1_raw, 2, 4, "w1_high")
-        w1_q = [packed(2 * P, "w1_low"), packed(2 * P, "w1_high")]
-        quantize(w1_q[0], 0, 2 * P, w1_low[:])
-        quantize(w1_q[1], 0, 2 * P, w1_high[:])
+        w1_low_q = packed(2 * P, "w1_low")
+        quantize(w1_low_q, 0, 2 * P, w1_low[:])
         half = S // 2
         for lo in (0, half):
             nc.vector.tensor_copy(
                 x_codes[:, lo : lo + half], x_word_table[:].bitcast(U32).indirect(entries(picks, lo, lo + half))
             )
         x_q = (x_codes, x_bytes)
+        w1_high_codes = keep.tile([P, 2 * P], U32, name="x_word_table", align_bytes=64)
+        w1_high_scales = keep.tile([P, 2 * P], U8, name="w1_high_scales", align_bytes=64)
+        w1_q = [w1_low_q, (w1_high_codes, w1_high_scales)]
+        quantize(w1_q[1], 0, 2 * P, w1_high[:])
 
         y_first = [psum.tile([P, half], F32, name=f"turn{u}") for u in range(2)]
         y_banks = [psum.tile([P, S], F32, name=f"bank{t}") for t in range(1, PACK)]
@@ -178,12 +181,12 @@ def tile_picked_joinminmxhingelap_none_p_kernel(tc, x_words, x_scales, w1, gn, g
         for t in range(PACK):
             d3 = d3_all[:, t * S : (t + 1) * S]
             nc.vector.tensor_tensor(d3, windows[t][:].indirect(list3[:]), neg_y[t][:], ALU.add)
-            nc.scalar.activation(hinge3[t], d3, ACT.Relu, scale=-2.0)
+            if t % 2 == 1:
+                both_tiles = slice((t - 1) * S, (t + 1) * S)
+                nc.scalar.activation(hinge_all[:, both_tiles], d3_all[:, both_tiles], ACT.Relu, scale=-2.0)
         w2_first, w3_first = packed(P, "w2_first"), packed(P, "w3_first")
-        z_q, z2_q = packed(S, "z"), packed(S, "z2")
         quantize(w2_first, 0, P, w2_grouped[:, : PACK * P])
         quantize(w3_first, 0, P, w3_grouped[:, : PACK * P])
-        quantize(z_q, 0, S, z_grouped[:])
 
         h_banks = [None] + [psum.tile([P, S], F32, name=f"bank{t}") for t in range(1, PACK)]
         neg_h = [keep.tile([P, S], F32, name=f"neg_h{t}", tag=f"neg_h{t}") for t in range(PACK)]
@@ -198,37 +201,45 @@ def tile_picked_joinminmxhingelap_none_p_kernel(tc, x_words, x_scales, w1, gn, g
 
         def finish_step(d4, lo, hi, t):
             width = hi - lo
-            both_tag = "z2_grouped0" if (lo, t) == (CHUNKS[1][0], 2) else f"both_{lo}_{t}"
-            both = keep.tile([P, width], F32, name="both", tag=both_tag, align_bytes=64)
+            both = keep.tile([P, width], F32, name=f"both_{lo}_{t}")
             nc.vector.scalar_tensor_tensor(both[:], d4[:], 0.0, hinge3[t][:, lo:hi], ALU.min, ALU.subtract)
             nc.scalar.activation(z2_planes[lo][:, t * width : (t + 1) * width], both[:], ACT.Copy, scale=z2_gain[:, t : t + 1])
             if t == PACK - 1:
-                h_first = psum.tile([P, width], F32, name="h_first", tag=bank_tags[lo])
-                quantize(z2_q, lo, hi, interleave(z2_planes[lo], f"z2_grouped{lo}")[:])
-                product(h_first[:], w2_first, 0, z_q, lo, hi, True, False)
-                product(h_first[:], w3_first, 0, z2_q, lo, hi, False, True)
-                nc.scalar.activation(windows[0][:, lo:hi], h_first[:], ACT.Copy, scale=0.75)
-                nc.scalar.activation(neg_h[0][:, lo:hi], h_first[:], ACT.Copy, scale=-1.0)
+                z2_grouped[lo] = interleave(z2_planes[lo], f"z2_grouped{lo}")
 
+        z2_grouped = {}
         fetched = fetch_gap4(*steps[0])
         for k, step in enumerate(steps):
             ahead = fetch_gap4(*steps[k + 1]) if k + 1 < len(steps) else None
             finish_step(fetched, *step)
             fetched = ahead
 
-        second_codes = trio.tile([P, 2 * P], U32, name="gap", align_bytes=64)
-        second_scales = keep.tile([P, 2 * P], U8, name="second_scales", align_bytes=64)
-        rest_codes = trio.tile([P, 4 * P], U32, name="gap", align_bytes=64)
-        rest_scales = keep.tile([P, 4 * P], U8, name="rest_scales", align_bytes=64)
-        second, rest = (second_codes, second_scales), (rest_codes, rest_scales)
-        quantize(second, 0, P, w2_grouped[:, PACK * P : 2 * PACK * P])
-        quantize(second, P, 2 * P, w3_grouped[:, PACK * P : 2 * PACK * P])
-        quantize(rest, 0, 2 * P, w2_grouped[:, 2 * PACK * P :])
-        quantize(rest, 2 * P, 4 * P, w3_grouped[:, 2 * PACK * P :])
+        hidden_codes = trio.tile([P, 2 * S], U32, name="gap", align_bytes=64)
+        hidden_scales = keep.tile([P, 2 * S], U8, name="hidden_scales", align_bytes=64)
+        hidden_q = (hidden_codes, hidden_scales)
+        quantize(hidden_q, 0, S, z_grouped[:])
+        h_first = {}
+        for lo, hi in CHUNKS:
+            h_first[lo] = psum.tile([P, hi - lo], F32, name="h_first", tag=bank_tags[lo])
+            quantize(hidden_q, S + lo, S + hi, z2_grouped[lo][:])
+            product(h_first[lo][:], w2_first, 0, hidden_q, lo, hi, True, False)
+            product(h_first[lo][:], w3_first, 0, hidden_q, S + lo, S + hi, False, True)
+            nc.scalar.activation(windows[0][:, lo:hi], h_first[lo][:], ACT.Copy, scale=0.75)
+            if lo == 0:
+                nc.scalar.activation(neg_h[0][:, lo:hi], h_first[lo][:], ACT.Copy, scale=-1.0)
+        for lo, hi in CHUNKS[1:]:
+            nc.scalar.activation(neg_h[0][:, lo:hi], h_first[lo][:], ACT.Copy, scale=-1.0)
+
+        rest_codes = keep.tile([P, 6 * P], U32, name="rest_codes", tag="z2_grouped384", align_bytes=64)
+        rest_scales = keep.tile([P, 6 * P], U8, name="rest_scales", align_bytes=64)
+        rest = (rest_codes, rest_scales)
+        quantize(rest, 0, P, w2_grouped[:, PACK * P : 2 * PACK * P])
+        quantize(rest, 3 * P, 4 * P, w3_grouped[:, PACK * P : 2 * PACK * P])
+        quantize(rest, P, 3 * P, w2_grouped[:, 2 * PACK * P :])
+        quantize(rest, 4 * P, 6 * P, w3_grouped[:, 2 * PACK * P :])
         for t in range(1, PACK):
-            left, m2, m3 = (second, 0, P) if t == 1 else (rest, (t - 2) * P, t * P)
-            product(h_banks[t][:], left, m2, z_q, 0, S, True, False)
-            product(h_banks[t][:], left, m3, z2_q, 0, S, False, True)
+            product(h_banks[t][:], rest, (t - 1) * P, hidden_q, 0, S, True, False)
+            product(h_banks[t][:], rest, (t + 2) * P, hidden_q, S, 2 * S, False, True)
             nc.scalar.activation(windows[t][:, :S], h_banks[t][:], ACT.Copy, scale=0.75)
             nc.scalar.activation(neg_h[t][:], h_banks[t][:], ACT.Copy, scale=-1.0)
 

@@ -30,8 +30,7 @@ def tile_picked_joinminmxhingelap_none_p_kernel(tc, x_words, x_scales, w1, gn, g
     nc = tc.nc
     with ExitStack() as ctx:
         keep = ctx.enter_context(tc.tile_pool(name="keep", bufs=1))
-        ring = ctx.enter_context(tc.tile_pool(name="ring", bufs=3))
-        trio = ctx.enter_context(tc.tile_pool(name="trio", bufs=3))
+        quad = ctx.enter_context(tc.tile_pool(name="quad", bufs=4))
         psum = ctx.enter_context(tc.psum_pool(name="psum", bufs=1))
 
         def load_list(src, name):
@@ -151,39 +150,43 @@ def tile_picked_joinminmxhingelap_none_p_kernel(tc, x_words, x_scales, w1, gn, g
         identity = keep.tile([P, P], F32, name="identity")
         make_identity(nc, identity[:])
         z_planes = keep.tile([P, PACK * S], BF16, name="z_planes")
-        d1_all = keep.tile([P, PACK * S], F32, name="wide_gap")
+        d2_low = keep.tile([P, PACK * half], F32, name="wide_gap")
         for t in range(PACK):
-            d1 = d1_all[:, t * S : (t + 1) * S]
-            d2 = [trio.tile([P, half], F32, name="gap", align_bytes=64) for lo in (0, half)]
-            shift = keep.tile([P, S], F32, name=f"shift{t}")
-            nc.vector.tensor_tensor(d2[0][:], windows[t][:].indirect(entries(list2, 0, half)), neg_y[t][:, :half], ALU.add)
-            nc.vector.tensor_tensor(d1, windows[t][:].indirect(list1[:]), neg_y[t][:], ALU.add)
-            nc.vector.tensor_tensor(d2[1][:], windows[t][:].indirect(entries(list2, half, S)), neg_y[t][:, half:], ALU.add)
+            d1 = keep.tile([P, S], F32, name=f"d1_{t}")
+            d2_high = keep.tile([P, half], F32, name=f"d2_high{t}")
+            d2 = [d2_low[:, t * half : (t + 1) * half], d2_high[:]]
+            if t < 2:
+                shift = [keep.tile([P, half], F32, name=f"shift{t}_{u}") for u in range(2)]
+            else:
+                shift = [quad.tile([P, half], F32, name="gap", align_bytes=64) for u in range(2)]
+            nc.vector.tensor_tensor(d2[0], windows[t][:].indirect(entries(list2, 0, half)), neg_y[t][:, :half], ALU.add)
+            nc.vector.tensor_tensor(d1[:], windows[t][:].indirect(list1[:]), neg_y[t][:], ALU.add)
+            nc.vector.tensor_tensor(d2[1], windows[t][:].indirect(entries(list2, half, S)), neg_y[t][:, half:], ALU.add)
             for lo in (0, half):
                 nc.vector.scalar_tensor_tensor(
-                    shift[:, lo : lo + half], d1[:, lo : lo + half], 0.0, d2[lo // half][:], ALU.max, ALU.min
+                    shift[lo // half][:], d1[:, lo : lo + half], 0.0, d2[lo // half], ALU.max, ALU.min
                 )
             turned = psum.tile([P, S], F32, name=f"turn{t % 2}")
             for c in range(0, S, P):
                 nc.tensor.matmul(turned[:, c : c + P], windows[t][:, c : c + P], identity[:], start=True, stop=False, is_transpose=True)
-                nc.tensor.matmul(turned[:, c : c + P], shift[:, c : c + P], identity[:], start=False, stop=True, is_transpose=True)
-            turned_sum = ring.tile([P, S], F32, name="turned_sum")
+                nc.tensor.matmul(turned[:, c : c + P], shift[c // half][:, c % half : c % half + P], identity[:], start=False, stop=True, is_transpose=True)
+            turned_sum = keep.tile([P, S], F32, name=f"turned_sum{t}")
             nc.scalar.copy(turned_sum[:], turned[:])
             back = psum.tile([P, S], F32, name=f"back{t % 2}")
             for c in range(0, S, P):
                 nc.tensor.transpose(back[:, c : c + P], turned_sum[:, c : c + P], identity[:])
             nc.scalar.activation(z_planes[:, t * S : (t + 1) * S], back[:], ACT.Copy, scale=gn_tile[:, t : t + 1])
-        z_grouped = interleave(z_planes, "z_grouped")
 
-        hinge_all = keep.tile([P, PACK * S], F32, name="z_planes")
-        hinge3 = [hinge_all[:, t * S : (t + 1) * S] for t in range(PACK)]
         d3_all = keep.tile([P, PACK * S], F32, name="wide_gap")
         for t in range(PACK):
             d3 = d3_all[:, t * S : (t + 1) * S]
             nc.vector.tensor_tensor(d3, windows[t][:].indirect(list3[:]), neg_y[t][:], ALU.add)
-            if t % 2 == 1:
-                both_tiles = slice((t - 1) * S, (t + 1) * S)
-                nc.scalar.activation(hinge_all[:, both_tiles], d3_all[:, both_tiles], ACT.Relu, scale=-2.0)
+        hinge_low = keep.tile([P, 2 * S], F32, name="turned_sum3")
+        nc.scalar.activation(hinge_low[:], d3_all[:, : 2 * S], ACT.Relu, scale=-2.0)
+        z_grouped = interleave(z_planes, "z_grouped")
+        hinge_high = keep.tile([P, 2 * S], F32, name="z_planes")
+        nc.scalar.activation(hinge_high[:], d3_all[:, 2 * S :], ACT.Relu, scale=-2.0)
+        hinge3 = [hinge_low[:, :S], hinge_low[:, S:], hinge_high[:, :S], hinge_high[:, S:]]
         w2_first, w3_first = packed(P, "w2_first"), packed(P, "w3_first")
         quantize(w2_first, 0, P, w2_grouped[:, : PACK * P])
         quantize(w3_first, 0, P, w3_grouped[:, : PACK * P])
@@ -192,10 +195,10 @@ def tile_picked_joinminmxhingelap_none_p_kernel(tc, x_words, x_scales, w1, gn, g
         neg_h = [keep.tile([P, S], F32, name=f"neg_h{t}", tag=f"neg_h{t}") for t in range(PACK)]
         steps = [(lo, hi, t) for lo, hi in CHUNKS for t in range(PACK)]
         bank_tags = {0: "turn0", 256: "turn1", 384: "bank0"}
-        z2_planes = {lo: keep.tile([P, PACK * (hi - lo)], BF16, name=f"z2_planes{lo}") for lo, hi in CHUNKS}
+        z2_planes = {lo: keep.tile([P, PACK * (hi - lo)], BF16, name="z2_planes", tag=f"z2_planes{lo}" if lo else "wide_gap") for lo, hi in CHUNKS}
 
         def fetch_gap4(lo, hi, t):
-            d4 = trio.tile([P, hi - lo], F32, name="gap", align_bytes=64)
+            d4 = quad.tile([P, hi - lo], F32, name="gap", align_bytes=64)
             nc.vector.tensor_tensor(d4[:], neg_y[t][:].indirect(entries(list4, lo, hi)), windows[t][:, lo:hi], ALU.add)
             return d4
 
@@ -214,7 +217,7 @@ def tile_picked_joinminmxhingelap_none_p_kernel(tc, x_words, x_scales, w1, gn, g
             finish_step(fetched, *step)
             fetched = ahead
 
-        hidden_codes = trio.tile([P, 2 * S], U32, name="gap", align_bytes=64)
+        hidden_codes = quad.tile([P, 2 * S], U32, name="gap", align_bytes=64)
         hidden_scales = keep.tile([P, 2 * S], U8, name="hidden_scales", align_bytes=64)
         hidden_q = (hidden_codes, hidden_scales)
         quantize(hidden_q, 0, S, z_grouped[:])

@@ -19,6 +19,10 @@ ACT = mybir.ActivationFunctionType
 P = 128
 PACK = 4
 STRIPE = 16
+QUADRANT = 32
+HALF = S // 2
+RUN = 4
+RING = 4
 CHUNKS = [(0, 256), (256, 384), (384, 512)]
 
 
@@ -26,11 +30,13 @@ def entries(offsets, lo, hi):
     return offsets[:, lo // STRIPE : hi // STRIPE]
 
 
-def tile_picked_joinminmxhingelap_none_p_kernel(tc, x_words, x_scales, w1, gn, gm, w2, w3, offs, n1, n2, n3, n4, n5, n6, out):
+def tile_picked_joinminmxhingelap_none_p_kernel(
+    tc, x_words, x_scales, w1, gn, gm, w2, w3, offs, n1, n2, n3, n4, n5, n6, out
+):
     nc = tc.nc
     with ExitStack() as ctx:
         keep = ctx.enter_context(tc.tile_pool(name="keep", bufs=1))
-        quad = ctx.enter_context(tc.tile_pool(name="quad", bufs=4))
+        ring = ctx.enter_context(tc.tile_pool(name="ring", bufs=RING))
         psum = ctx.enter_context(tc.psum_pool(name="psum", bufs=1))
 
         def load_list(src, name):
@@ -56,20 +62,19 @@ def tile_picked_joinminmxhingelap_none_p_kernel(tc, x_words, x_scales, w1, gn, g
         def quantize(dest, lo, hi, grouped):
             nc.vector.quantize_mx(out=dest[0][:, lo:hi].bitcast(FP8X4), scales=dest[1][:, lo:hi], in_=grouped)
 
-        def deal_weight(copy, raw, t0, t1, name):
+        def deal_weight(raw, t0, t1, name):
             grouped = keep.tile([P, (t1 - t0) * P * PACK], BF16, name=name, align_bytes=64)
-            copy(
+            nc.scalar.copy(
                 grouped[:].rearrange("p (t m j) -> p m j t", m=P, j=PACK),
                 raw[:].rearrange("p (j m t) -> p m j t", j=PACK, t=PACK)[:, :, :, t0:t1],
             )
             return grouped
 
         def interleave(planes, name):
-            width = planes.shape[1] // PACK
-            grouped = keep.tile([P, PACK * width], BF16, name=name, tag=name, align_bytes=64)
+            grouped = keep.tile([P, planes.shape[1]], BF16, name=name, tag=name, align_bytes=64)
             nc.scalar.copy(
-                grouped[:].rearrange("p (c i t) -> p c t i", i=4, t=PACK),
-                planes[:].rearrange("p (t c i) -> p c t i", t=PACK, i=4),
+                grouped[:].rearrange("p (c i t) -> p c t i", i=RUN, t=PACK),
+                planes.rearrange("p (t c i) -> p c t i", t=PACK, i=RUN),
             )
             return grouped
 
@@ -88,12 +93,12 @@ def tile_picked_joinminmxhingelap_none_p_kernel(tc, x_words, x_scales, w1, gn, g
         nc.vector.memset(x_scale_table[:].bitcast(I32), 0)
         w1_raw = load_weight(w1, "w1_raw")
         picks = load_list(offs, "picks")
-        for q in range(4):
+        for q in range(P // QUADRANT):
             nc.sync.dma_start(
-                x_scale_table[32 * q : 32 * q + 4, :].bitcast(I32),
+                x_scale_table[QUADRANT * q : QUADRANT * q + 4, :].bitcast(I32),
                 x_scales[0, 4 * q : 4 * q + 4, :].bitcast(I32),
             )
-        x_word_table = keep.tile([P, T], I32, name="x_word_table", align_bytes=64)
+        x_word_table = keep.tile([P, T], I32, name="x_word_table", tag="x_word_table", align_bytes=64)
         nc.sync.dma_start(x_word_table[:], x_words[0].rearrange("p c r -> p (c r)").bitcast(I32))
         gm_tile = load_gain(gm, "gm_tile")
         list2 = load_list(n2, "list2")
@@ -116,27 +121,26 @@ def tile_picked_joinminmxhingelap_none_p_kernel(tc, x_words, x_scales, w1, gn, g
         x_codes = keep.tile([P, S], U32, name="x_codes", align_bytes=64)
         x_bytes = keep.tile([P, S], U8, name="x_bytes", align_bytes=64)
         nc.vector.tensor_copy(x_bytes[:], x_scale_table[:].indirect(picks[:]))
-        w1_low = deal_weight(nc.scalar.copy, w1_raw, 0, 2, "w1_low")
-        w1_high = deal_weight(nc.scalar.copy, w1_raw, 2, 4, "w1_high")
+        w1_low = deal_weight(w1_raw, 0, 2, "w1_low")
+        w1_high = deal_weight(w1_raw, 2, 4, "w1_high")
         w1_low_q = packed(2 * P, "w1_low")
         quantize(w1_low_q, 0, 2 * P, w1_low[:])
-        half = S // 2
-        for lo in (0, half):
+        for lo in (0, HALF):
             nc.vector.tensor_copy(
-                x_codes[:, lo : lo + half], x_word_table[:].bitcast(U32).indirect(entries(picks, lo, lo + half))
+                x_codes[:, lo : lo + HALF], x_word_table[:].bitcast(U32).indirect(entries(picks, lo, lo + HALF))
             )
         x_q = (x_codes, x_bytes)
-        w1_high_codes = keep.tile([P, 2 * P], U32, name="x_word_table", align_bytes=64)
+        w1_high_codes = keep.tile([P, 2 * P], U32, name="w1_high_codes", tag="x_word_table", align_bytes=64)
         w1_high_scales = keep.tile([P, 2 * P], U8, name="w1_high_scales", align_bytes=64)
         w1_q = [w1_low_q, (w1_high_codes, w1_high_scales)]
         quantize(w1_q[1], 0, 2 * P, w1_high[:])
 
-        y_first = [psum.tile([P, half], F32, name=f"turn{u}") for u in range(2)]
-        y_banks = [psum.tile([P, S], F32, name=f"bank{t}") for t in range(1, PACK)]
+        y_first = [psum.tile([P, HALF], F32, name="y_first", tag=f"turn{u}") for u in range(2)]
+        y_banks = [psum.tile([P, S], F32, name="y_bank", tag=f"bank{t}") for t in range(1, PACK)]
         neg_y = [keep.tile([P, S], F32, name=f"neg_y{t}") for t in range(PACK)]
         for u in range(2):
-            cols = slice(u * half, (u + 1) * half)
-            product(y_first[u][:], w1_q[0], 0, x_q, u * half, (u + 1) * half, True, True)
+            cols = slice(u * HALF, (u + 1) * HALF)
+            product(y_first[u][:], w1_q[0], 0, x_q, u * HALF, (u + 1) * HALF, True, True)
             nc.scalar.copy(windows[0][:, cols], y_first[u][:])
             nc.scalar.activation(neg_y[0][:, cols], y_first[u][:], ACT.Copy, scale=-1.0)
         for t in range(1, PACK):
@@ -144,86 +148,90 @@ def tile_picked_joinminmxhingelap_none_p_kernel(tc, x_words, x_scales, w1, gn, g
             nc.scalar.copy(windows[t][:, :S], y_banks[t - 1][:])
             nc.scalar.activation(neg_y[t][:], y_banks[t - 1][:], ACT.Copy, scale=-1.0)
 
-        w2_grouped = deal_weight(nc.scalar.copy, w2_raw, 0, PACK, "w2_grouped")
-        w3_grouped = deal_weight(nc.scalar.copy, w3_raw, 0, PACK, "w3_grouped")
+        w2_grouped = deal_weight(w2_raw, 0, PACK, "w2_grouped")
+        w3_grouped = deal_weight(w3_raw, 0, PACK, "w3_grouped")
 
         identity = keep.tile([P, P], F32, name="identity")
         make_identity(nc, identity[:])
-        z_planes = keep.tile([P, PACK * S], BF16, name="z_planes")
-        d2_low = keep.tile([P, PACK * half], F32, name="wide_gap")
+        z_planes = keep.tile([P, PACK * S], BF16, name="z_planes", tag="z_planes")
+        d2_low = keep.tile([P, PACK * HALF], F32, name="d2_low", tag="wide")
         for t in range(PACK):
             d1 = keep.tile([P, S], F32, name=f"d1_{t}")
-            d2_high = keep.tile([P, half], F32, name=f"d2_high{t}")
-            d2 = [d2_low[:, t * half : (t + 1) * half], d2_high[:]]
-            if t < 2:
-                shift = [keep.tile([P, half], F32, name=f"shift{t}_{u}") for u in range(2)]
+            d2_high = keep.tile([P, HALF], F32, name=f"d2_high{t}")
+            d2 = [d2_low[:, t * HALF : (t + 1) * HALF], d2_high[:]]
+            if t < PACK - RING // 2:
+                shift = [keep.tile([P, HALF], F32, name=f"shift{t}_{u}") for u in range(2)]
             else:
-                shift = [quad.tile([P, half], F32, name="gap", align_bytes=64) for u in range(2)]
-            nc.vector.tensor_tensor(d2[0], windows[t][:].indirect(entries(list2, 0, half)), neg_y[t][:, :half], ALU.add)
+                shift = [ring.tile([P, HALF], F32, name="shift", tag="slot", align_bytes=64) for u in range(2)]
+            nc.vector.tensor_tensor(d2[0], windows[t][:].indirect(entries(list2, 0, HALF)), neg_y[t][:, :HALF], ALU.add)
             nc.vector.tensor_tensor(d1[:], windows[t][:].indirect(list1[:]), neg_y[t][:], ALU.add)
-            nc.vector.tensor_tensor(d2[1], windows[t][:].indirect(entries(list2, half, S)), neg_y[t][:, half:], ALU.add)
-            for lo in (0, half):
+            nc.vector.tensor_tensor(d2[1], windows[t][:].indirect(entries(list2, HALF, S)), neg_y[t][:, HALF:], ALU.add)
+            for u in range(2):
                 nc.vector.scalar_tensor_tensor(
-                    shift[lo // half][:], d1[:, lo : lo + half], 0.0, d2[lo // half], ALU.max, ALU.min
+                    shift[u][:], d1[:, u * HALF : (u + 1) * HALF], 0.0, d2[u], ALU.max, ALU.min
                 )
-            turned = psum.tile([P, S], F32, name=f"turn{t % 2}")
+            turned = psum.tile([P, S], F32, name="turned", tag=f"turn{t % 2}")
             for c in range(0, S, P):
-                nc.tensor.matmul(turned[:, c : c + P], windows[t][:, c : c + P], identity[:], start=True, stop=False, is_transpose=True)
-                nc.tensor.matmul(turned[:, c : c + P], shift[c // half][:, c % half : c % half + P], identity[:], start=False, stop=True, is_transpose=True)
-            turned_sum = keep.tile([P, S], F32, name=f"turned_sum{t}")
+                block = turned[:, c : c + P]
+                shift_block = shift[c // HALF][:, c % HALF : c % HALF + P]
+                nc.tensor.matmul(block, windows[t][:, c : c + P], identity[:], start=True, stop=False, is_transpose=True)
+                nc.tensor.matmul(block, shift_block, identity[:], start=False, stop=True, is_transpose=True)
+            turned_sum = keep.tile([P, S], F32, name="turned_sum", tag=f"turned_sum{t}")
             nc.scalar.copy(turned_sum[:], turned[:])
-            back = psum.tile([P, S], F32, name=f"back{t % 2}")
+            back = psum.tile([P, S], F32, name="back", tag=f"back{t % 2}")
             for c in range(0, S, P):
                 nc.tensor.transpose(back[:, c : c + P], turned_sum[:, c : c + P], identity[:])
             nc.scalar.activation(z_planes[:, t * S : (t + 1) * S], back[:], ACT.Copy, scale=gn_tile[:, t : t + 1])
 
-        d3_all = keep.tile([P, PACK * S], F32, name="wide_gap")
+        d3 = keep.tile([P, PACK * S], F32, name="d3", tag="wide")
         for t in range(PACK):
-            d3 = d3_all[:, t * S : (t + 1) * S]
-            nc.vector.tensor_tensor(d3, windows[t][:].indirect(list3[:]), neg_y[t][:], ALU.add)
-        hinge_low = keep.tile([P, 2 * S], F32, name="turned_sum3")
-        nc.scalar.activation(hinge_low[:], d3_all[:, : 2 * S], ACT.Relu, scale=-2.0)
-        z_grouped = interleave(z_planes, "z_grouped")
-        hinge_high = keep.tile([P, 2 * S], F32, name="z_planes")
-        nc.scalar.activation(hinge_high[:], d3_all[:, 2 * S :], ACT.Relu, scale=-2.0)
-        hinge3 = [hinge_low[:, :S], hinge_low[:, S:], hinge_high[:, :S], hinge_high[:, S:]]
+            nc.vector.tensor_tensor(d3[:, t * S : (t + 1) * S], windows[t][:].indirect(list3[:]), neg_y[t][:], ALU.add)
+        hinge_low = keep.tile([P, 2 * S], F32, name="hinge_low", tag=f"turned_sum{PACK - 1}")
+        nc.scalar.activation(hinge_low[:], d3[:, : 2 * S], ACT.Relu, scale=-2.0)
+        z_grouped = interleave(z_planes[:], "z_grouped")
+        hinge_high = keep.tile([P, 2 * S], F32, name="hinge_high", tag="z_planes")
+        nc.scalar.activation(hinge_high[:], d3[:, 2 * S :], ACT.Relu, scale=-2.0)
+        hinge = [hinge_low[:, :S], hinge_low[:, S:], hinge_high[:, :S], hinge_high[:, S:]]
         w2_first, w3_first = packed(P, "w2_first"), packed(P, "w3_first")
         quantize(w2_first, 0, P, w2_grouped[:, : PACK * P])
         quantize(w3_first, 0, P, w3_grouped[:, : PACK * P])
 
-        h_banks = [None] + [psum.tile([P, S], F32, name=f"bank{t}") for t in range(1, PACK)]
-        neg_h = [keep.tile([P, S], F32, name=f"neg_h{t}", tag=f"neg_h{t}") for t in range(PACK)]
-        steps = [(lo, hi, t) for lo, hi in CHUNKS for t in range(PACK)]
-        bank_tags = {0: "turn0", 256: "turn1", 384: "bank0"}
-        z2_planes = {lo: keep.tile([P, PACK * (hi - lo)], BF16, name="z2_planes", tag=f"z2_planes{lo}" if lo else "wide_gap") for lo, hi in CHUNKS}
+        h_banks = {t: psum.tile([P, S], F32, name="h_bank", tag=f"bank{t}") for t in range(1, PACK)}
+        neg_h = [keep.tile([P, S], F32, name=f"neg_h{t}") for t in range(PACK)]
 
-        def fetch_gap4(lo, hi, t):
-            d4 = quad.tile([P, hi - lo], F32, name="gap", align_bytes=64)
-            nc.vector.tensor_tensor(d4[:], neg_y[t][:].indirect(entries(list4, lo, hi)), windows[t][:, lo:hi], ALU.add)
-            return d4
+        z2_planes_all = keep.tile([P, PACK * S], BF16, name="z2_planes_all", tag="wide")
+        z2_planes = {lo: z2_planes_all[:, PACK * lo : PACK * hi] for lo, hi in CHUNKS}
+        z2_grouped = {}
 
-        def finish_step(d4, lo, hi, t):
+        def fetch_neg_d4(lo, hi, t):
+            neg_d4 = ring.tile([P, hi - lo], F32, name="neg_d4", tag="slot", align_bytes=64)
+            nc.vector.tensor_tensor(neg_d4[:], neg_y[t][:].indirect(entries(list4, lo, hi)), windows[t][:, lo:hi], ALU.add)
+            return neg_d4
+
+        def finish_z2(neg_d4, lo, hi, t):
             width = hi - lo
-            both = keep.tile([P, width], F32, name=f"both_{lo}_{t}")
-            nc.vector.scalar_tensor_tensor(both[:], d4[:], 0.0, hinge3[t][:, lo:hi], ALU.min, ALU.subtract)
-            nc.scalar.activation(z2_planes[lo][:, t * width : (t + 1) * width], both[:], ACT.Copy, scale=z2_gain[:, t : t + 1])
+            terms = keep.tile([P, width], F32, name=f"terms_{lo}_{t}")
+            nc.vector.scalar_tensor_tensor(terms[:], neg_d4[:], 0.0, hinge[t][:, lo:hi], ALU.min, ALU.subtract)
+            nc.scalar.activation(
+                z2_planes[lo][:, t * width : (t + 1) * width], terms[:], ACT.Copy, scale=z2_gain[:, t : t + 1]
+            )
             if t == PACK - 1:
                 z2_grouped[lo] = interleave(z2_planes[lo], f"z2_grouped{lo}")
 
-        z2_grouped = {}
-        fetched = fetch_gap4(*steps[0])
+        steps = [(lo, hi, t) for lo, hi in CHUNKS for t in range(PACK)]
+        fetched = fetch_neg_d4(*steps[0])
         for k, step in enumerate(steps):
-            ahead = fetch_gap4(*steps[k + 1]) if k + 1 < len(steps) else None
-            finish_step(fetched, *step)
+            ahead = fetch_neg_d4(*steps[k + 1]) if k + 1 < len(steps) else None
+            finish_z2(fetched, *step)
             fetched = ahead
 
-        hidden_codes = quad.tile([P, 2 * S], U32, name="gap", align_bytes=64)
+        hidden_codes = ring.tile([P, 2 * S], U32, name="hidden_codes", tag="slot", align_bytes=64)
         hidden_scales = keep.tile([P, 2 * S], U8, name="hidden_scales", align_bytes=64)
         hidden_q = (hidden_codes, hidden_scales)
         quantize(hidden_q, 0, S, z_grouped[:])
         h_first = {}
-        for lo, hi in CHUNKS:
-            h_first[lo] = psum.tile([P, hi - lo], F32, name="h_first", tag=bank_tags[lo])
+        for (lo, hi), bank_tag in zip(CHUNKS, ("turn0", "turn1", "bank0")):
+            h_first[lo] = psum.tile([P, hi - lo], F32, name="h_first", tag=bank_tag)
             quantize(hidden_q, S + lo, S + hi, z2_grouped[lo][:])
             product(h_first[lo][:], w2_first, 0, hidden_q, lo, hi, True, False)
             product(h_first[lo][:], w3_first, 0, hidden_q, S + lo, S + hi, False, True)
@@ -233,16 +241,16 @@ def tile_picked_joinminmxhingelap_none_p_kernel(tc, x_words, x_scales, w1, gn, g
         for lo, hi in CHUNKS[1:]:
             nc.scalar.activation(neg_h[0][:, lo:hi], h_first[lo][:], ACT.Copy, scale=-1.0)
 
-        rest_codes = keep.tile([P, 6 * P], U32, name="rest_codes", tag="z2_grouped384", align_bytes=64)
-        rest_scales = keep.tile([P, 6 * P], U8, name="rest_scales", align_bytes=64)
-        rest = (rest_codes, rest_scales)
-        quantize(rest, 0, P, w2_grouped[:, PACK * P : 2 * PACK * P])
-        quantize(rest, 3 * P, 4 * P, w3_grouped[:, PACK * P : 2 * PACK * P])
-        quantize(rest, P, 3 * P, w2_grouped[:, 2 * PACK * P :])
-        quantize(rest, 4 * P, 6 * P, w3_grouped[:, 2 * PACK * P :])
+        rest_width = (PACK - 1) * P
+        rest_codes = keep.tile([P, 2 * rest_width], U32, name="rest_codes", tag=f"z2_grouped{CHUNKS[-1][0]}", align_bytes=64)
+        rest_scales = keep.tile([P, 2 * rest_width], U8, name="rest_scales", align_bytes=64)
+        rest_q = (rest_codes, rest_scales)
+        for t0, t1 in ((1, 2), (2, PACK)):
+            for base, grouped in ((0, w2_grouped), (rest_width, w3_grouped)):
+                quantize(rest_q, base + (t0 - 1) * P, base + (t1 - 1) * P, grouped[:, t0 * PACK * P : t1 * PACK * P])
         for t in range(1, PACK):
-            product(h_banks[t][:], rest, (t - 1) * P, hidden_q, 0, S, True, False)
-            product(h_banks[t][:], rest, (t + 2) * P, hidden_q, S, 2 * S, False, True)
+            product(h_banks[t][:], rest_q, (t - 1) * P, hidden_q, 0, S, True, False)
+            product(h_banks[t][:], rest_q, rest_width + (t - 1) * P, hidden_q, S, 2 * S, False, True)
             nc.scalar.activation(windows[t][:, :S], h_banks[t][:], ACT.Copy, scale=0.75)
             nc.scalar.activation(neg_h[t][:], h_banks[t][:], ACT.Copy, scale=-1.0)
 
@@ -250,12 +258,14 @@ def tile_picked_joinminmxhingelap_none_p_kernel(tc, x_words, x_scales, w1, gn, g
         for t in range(PACK):
             partial = keep.tile([P, S], F32, name=f"partial{t}")
             result = keep.tile([P, S], F32, name=f"result{t}")
-            for lo in (0, half):
-                cols = slice(lo, lo + half)
-                nc.vector.tensor_tensor(partial[:, cols], windows[t][:].indirect(entries(list5, lo, lo + half)), neg_h[t][:, cols], ALU.add)
-            for lo in (0, half):
-                cols = slice(lo, lo + half)
-                nc.vector.tensor_tensor(result[:, cols], windows[t][:].indirect(entries(list6, lo, lo + half)), partial[:, cols], ALU.add)
+            for lo in (0, HALF):
+                cols = slice(lo, lo + HALF)
+                looked_up = windows[t][:].indirect(entries(list5, lo, lo + HALF))
+                nc.vector.tensor_tensor(partial[:, cols], looked_up, neg_h[t][:, cols], ALU.add)
+            for lo in (0, HALF):
+                cols = slice(lo, lo + HALF)
+                looked_up = windows[t][:].indirect(entries(list6, lo, lo + HALF))
+                nc.vector.tensor_tensor(result[:, cols], looked_up, partial[:, cols], ALU.add)
                 if t == PACK - 1:
                     nc.sync.dma_start(out_rows[:, t, cols], result[:, cols])
             if t < PACK - 1:

from contextlib import ExitStack

import concourse.mybir as mybir
from concourse.masks import make_identity

K, T, S, H, N = 512, 2048, 512, 512, 512
FLOPS = 2 * K * H * S + 2 * 2 * H * N * S

F32 = mybir.dt.float32
BF16 = mybir.dt.bfloat16
I32 = mybir.dt.int32
U32 = mybir.dt.uint32
U16 = mybir.dt.uint16
U8 = mybir.dt.uint8
FP8X4 = mybir.dt.float8_e4m3fn_x4
ALU = mybir.AluOpType
ACT = mybir.ActivationFunctionType

P = 128
PACK = 4
STRIPE = 16
QUADRANT = 32
HALF = S // 2
RUN = 4
RING = 4
CHUNKS = [(0, 256), (256, 384), (384, 512)]


def entries(offsets, lo, hi):
    return offsets[:, lo // STRIPE : hi // STRIPE]


def tile_picked_joinminmxhingelap_none_p_kernel(
    tc, x_words, x_scales, w1, gn, gm, w2, w3, offs, n1, n2, n3, n4, n5, n6, out
):
    nc = tc.nc
    with ExitStack() as ctx:
        keep = ctx.enter_context(tc.tile_pool(name="keep", bufs=1))
        ring = ctx.enter_context(tc.tile_pool(name="ring", bufs=RING))
        psum = ctx.enter_context(tc.psum_pool(name="psum", bufs=1))

        def load_list(src, name):
            tile = keep.tile([P, S // STRIPE], U16, name=name)
            nc.sync.dma_start(tile[:], src)
            return tile

        def load_weight(src, name):
            tile = keep.tile([P, PACK * src.shape[1]], F32, name=name)
            nc.sync.dma_start(tile[:], src.rearrange("(p j) c -> p (j c)", j=PACK))
            return tile

        def load_gain(src, name):
            tile = keep.tile([P, PACK], F32, name=name)
            nc.sync.dma_start(tile[:], src.rearrange("(p t) o -> p (t o)", t=PACK))
            return tile

        def packed(width, name):
            codes = keep.tile([P, width], U32, name=name + "_codes", align_bytes=64)
            scales = keep.tile([P, width], U8, name=name + "_scales", align_bytes=64)
            return codes, scales

        def quantize(dest, lo, hi, grouped):
            nc.vector.quantize_mx(out=dest[0][:, lo:hi].bitcast(FP8X4), scales=dest[1][:, lo:hi], in_=grouped)

        def deal_weight(raw, t0, t1, name):
            grouped = keep.tile([P, (t1 - t0) * P * PACK], BF16, name=name, align_bytes=64)
            nc.scalar.copy(
                grouped[:].rearrange("p (t m j) -> p m j t", m=P, j=PACK),
                raw[:].rearrange("p (j m t) -> p m j t", j=PACK, t=PACK)[:, :, :, t0:t1],
            )
            return grouped

        def interleave(planes, name):
            grouped = keep.tile([P, planes.shape[1]], BF16, name=name, tag=name, align_bytes=64)
            nc.scalar.copy(
                grouped[:].rearrange("p (c i t) -> p c t i", i=RUN, t=PACK),
                planes.rearrange("p (t c i) -> p c t i", t=PACK, i=RUN),
            )
            return grouped

        def product(acc, left, m0, right, lo, hi, start, stop):
            nc.tensor.matmul_mx(
                out=acc,
                lhsT=left[0][:, m0 : m0 + P].bitcast(FP8X4),
                lhsT_scale=left[1][:, m0 : m0 + P],
                rhs=right[0][:, lo:hi].bitcast(FP8X4),
                rhs_scale=right[1][:, lo:hi],
                start=start,
                stop=stop,
            )

        x_scale_table = keep.tile([P, T], U8, name="x_scale_table")
        nc.vector.memset(x_scale_table[:].bitcast(I32), 0)
        w1_raw = load_weight(w1, "w1_raw")
        picks = load_list(offs, "picks")
        for q in range(P // QUADRANT):
            nc.sync.dma_start(
                x_scale_table[QUADRANT * q : QUADRANT * q + 4, :].bitcast(I32),
                x_scales[0, 4 * q : 4 * q + 4, :].bitcast(I32),
            )
        x_word_table = keep.tile([P, T], I32, name="x_word_table", tag="x_word_table", align_bytes=64)
        nc.sync.dma_start(x_word_table[:], x_words[0].rearrange("p c r -> p (c r)").bitcast(I32))
        gm_tile = load_gain(gm, "gm_tile")
        list2 = load_list(n2, "list2")
        list1 = load_list(n1, "list1")
        gn_tile = load_gain(gn, "gn_tile")
        list3 = load_list(n3, "list3")
        w2_raw = load_weight(w2, "w2_raw")
        w3_raw = load_weight(w3, "w3_raw")
        list4 = load_list(n4, "list4")
        list5 = load_list(n5, "list5")
        list6 = load_list(n6, "list6")

        windows = [keep.tile([P, 2 * S], F32, name=f"window{t}") for t in range(PACK)]
        for t in range(PACK):
            nc.vector.memset(windows[t][:, S:], 0.0)

        z2_gain = keep.tile([P, PACK], F32, name="z2_gain")
        nc.scalar.activation(z2_gain[:], gm_tile[:], ACT.Copy, scale=-0.5)

        x_codes = keep.tile([P, S], U32, name="x_codes", align_bytes=64)
        x_bytes = keep.tile([P, S], U8, name="x_bytes", align_bytes=64)
        nc.vector.tensor_copy(x_bytes[:], x_scale_table[:].indirect(picks[:]))
        w1_low = deal_weight(w1_raw, 0, 2, "w1_low")
        w1_high = deal_weight(w1_raw, 2, 4, "w1_high")
        w1_low_q = packed(2 * P, "w1_low")
        quantize(w1_low_q, 0, 2 * P, w1_low[:])
        for lo in (0, HALF):
            nc.vector.tensor_copy(
                x_codes[:, lo : lo + HALF], x_word_table[:].bitcast(U32).indirect(entries(picks, lo, lo + HALF))
            )
        x_q = (x_codes, x_bytes)
        w1_high_codes = keep.tile([P, 2 * P], U32, name="w1_high_codes", tag="x_word_table", align_bytes=64)
        w1_high_scales = keep.tile([P, 2 * P], U8, name="w1_high_scales", align_bytes=64)
        w1_q = [w1_low_q, (w1_high_codes, w1_high_scales)]
        quantize(w1_q[1], 0, 2 * P, w1_high[:])

        y_first = [psum.tile([P, HALF], F32, name="y_first", tag=f"turn{u}") for u in range(2)]
        y_banks = [psum.tile([P, S], F32, name="y_bank", tag=f"bank{t}") for t in range(1, PACK)]
        neg_y = [keep.tile([P, S], F32, name=f"neg_y{t}") for t in range(PACK)]
        for u in range(2):
            cols = slice(u * HALF, (u + 1) * HALF)
            product(y_first[u][:], w1_q[0], 0, x_q, u * HALF, (u + 1) * HALF, True, True)
            nc.scalar.copy(windows[0][:, cols], y_first[u][:])
            nc.scalar.activation(neg_y[0][:, cols], y_first[u][:], ACT.Copy, scale=-1.0)
        for t in range(1, PACK):
            product(y_banks[t - 1][:], w1_q[t // 2], (t % 2) * P, x_q, 0, S, True, True)
            nc.scalar.copy(windows[t][:, :S], y_banks[t - 1][:])
            nc.scalar.activation(neg_y[t][:], y_banks[t - 1][:], ACT.Copy, scale=-1.0)

        w2_grouped = deal_weight(w2_raw, 0, PACK, "w2_grouped")
        w3_grouped = deal_weight(w3_raw, 0, PACK, "w3_grouped")

        identity = keep.tile([P, P], F32, name="identity")
        make_identity(nc, identity[:])
        z_planes = keep.tile([P, PACK * S], BF16, name="z_planes", tag="z_planes")
        d2_low = keep.tile([P, PACK * HALF], F32, name="d2_low", tag="wide")
        for t in range(PACK):
            d1 = keep.tile([P, S], F32, name=f"d1_{t}")
            d2_high = keep.tile([P, HALF], F32, name=f"d2_high{t}")
            d2 = [d2_low[:, t * HALF : (t + 1) * HALF], d2_high[:]]
            if t < PACK - RING // 2:
                shift = [keep.tile([P, HALF], F32, name=f"shift{t}_{u}") for u in range(2)]
            else:
                shift = [ring.tile([P, HALF], F32, name="shift", tag="slot", align_bytes=64) for u in range(2)]
            nc.vector.tensor_tensor(d2[0], windows[t][:].indirect(entries(list2, 0, HALF)), neg_y[t][:, :HALF], ALU.add)
            nc.vector.tensor_tensor(d1[:], windows[t][:].indirect(list1[:]), neg_y[t][:], ALU.add)
            nc.vector.tensor_tensor(d2[1], windows[t][:].indirect(entries(list2, HALF, S)), neg_y[t][:, HALF:], ALU.add)
            for u in range(2):
                nc.vector.scalar_tensor_tensor(
                    shift[u][:], d1[:, u * HALF : (u + 1) * HALF], 0.0, d2[u], ALU.max, ALU.min
                )
            turned = psum.tile([P, S], F32, name="turned", tag=f"turn{t % 2}")
            for c in range(0, S, P):
                block = turned[:, c : c + P]
                shift_block = shift[c // HALF][:, c % HALF : c % HALF + P]
                nc.tensor.matmul(block, windows[t][:, c : c + P], identity[:], start=True, stop=False, is_transpose=True)
                nc.tensor.matmul(block, shift_block, identity[:], start=False, stop=True, is_transpose=True)
            turned_sum = keep.tile([P, S], F32, name="turned_sum", tag=f"turned_sum{t}")
            nc.scalar.copy(turned_sum[:], turned[:])
            back = psum.tile([P, S], F32, name="back", tag=f"back{t % 2}")
            for c in range(0, S, P):
                nc.tensor.transpose(back[:, c : c + P], turned_sum[:, c : c + P], identity[:])
            nc.scalar.activation(z_planes[:, t * S : (t + 1) * S], back[:], ACT.Copy, scale=gn_tile[:, t : t + 1])

        d3 = keep.tile([P, PACK * S], F32, name="d3", tag="wide")
        for t in range(PACK):
            nc.vector.tensor_tensor(d3[:, t * S : (t + 1) * S], windows[t][:].indirect(list3[:]), neg_y[t][:], ALU.add)
        hinge_low = keep.tile([P, 2 * S], F32, name="hinge_low", tag=f"turned_sum{PACK - 1}")
        nc.scalar.activation(hinge_low[:], d3[:, : 2 * S], ACT.Relu, scale=-2.0)
        z_grouped = interleave(z_planes[:], "z_grouped")
        hinge_high = keep.tile([P, 2 * S], F32, name="hinge_high", tag="z_planes")
        nc.scalar.activation(hinge_high[:], d3[:, 2 * S :], ACT.Relu, scale=-2.0)
        hinge = [hinge_low[:, :S], hinge_low[:, S:], hinge_high[:, :S], hinge_high[:, S:]]
        w2_first, w3_first = packed(P, "w2_first"), packed(P, "w3_first")
        quantize(w2_first, 0, P, w2_grouped[:, : PACK * P])
        quantize(w3_first, 0, P, w3_grouped[:, : PACK * P])

        h_banks = {t: psum.tile([P, S], F32, name="h_bank", tag=f"bank{t}") for t in range(1, PACK)}
        neg_h = [keep.tile([P, S], F32, name=f"neg_h{t}") for t in range(PACK)]

        z2_planes_all = keep.tile([P, PACK * S], BF16, name="z2_planes_all", tag="wide")
        z2_planes = {lo: z2_planes_all[:, PACK * lo : PACK * hi] for lo, hi in CHUNKS}
        z2_grouped = {}

        def fetch_neg_d4(lo, hi, t):
            neg_d4 = ring.tile([P, hi - lo], F32, name="neg_d4", tag="slot", align_bytes=64)
            nc.vector.tensor_tensor(neg_d4[:], neg_y[t][:].indirect(entries(list4, lo, hi)), windows[t][:, lo:hi], ALU.add)
            return neg_d4

        def finish_z2(neg_d4, lo, hi, t):
            width = hi - lo
            terms = keep.tile([P, width], F32, name=f"terms_{lo}_{t}")
            nc.vector.scalar_tensor_tensor(terms[:], neg_d4[:], 0.0, hinge[t][:, lo:hi], ALU.min, ALU.subtract)
            nc.scalar.activation(
                z2_planes[lo][:, t * width : (t + 1) * width], terms[:], ACT.Copy, scale=z2_gain[:, t : t + 1]
            )
            if t == PACK - 1:
                z2_grouped[lo] = interleave(z2_planes[lo], f"z2_grouped{lo}")

        steps = [(lo, hi, t) for lo, hi in CHUNKS for t in range(PACK)]
        fetched = fetch_neg_d4(*steps[0])
        for k, step in enumerate(steps):
            ahead = fetch_neg_d4(*steps[k + 1]) if k + 1 < len(steps) else None
            finish_z2(fetched, *step)
            fetched = ahead

        hidden_codes = ring.tile([P, 2 * S], U32, name="hidden_codes", tag="slot", align_bytes=64)
        hidden_scales = keep.tile([P, 2 * S], U8, name="hidden_scales", align_bytes=64)
        hidden_q = (hidden_codes, hidden_scales)
        quantize(hidden_q, 0, S, z_grouped[:])
        h_first = {}
        for (lo, hi), bank_tag in zip(CHUNKS, ("turn0", "turn1", "bank0")):
            h_first[lo] = psum.tile([P, hi - lo], F32, name="h_first", tag=bank_tag)
            quantize(hidden_q, S + lo, S + hi, z2_grouped[lo][:])
            product(h_first[lo][:], w2_first, 0, hidden_q, lo, hi, True, False)
            product(h_first[lo][:], w3_first, 0, hidden_q, S + lo, S + hi, False, True)
            nc.scalar.activation(windows[0][:, lo:hi], h_first[lo][:], ACT.Copy, scale=0.75)
            if lo == 0:
                nc.scalar.activation(neg_h[0][:, lo:hi], h_first[lo][:], ACT.Copy, scale=-1.0)
        for lo, hi in CHUNKS[1:]:
            nc.scalar.activation(neg_h[0][:, lo:hi], h_first[lo][:], ACT.Copy, scale=-1.0)

        rest_width = (PACK - 1) * P
        rest_codes = keep.tile([P, 2 * rest_width], U32, name="rest_codes", tag=f"z2_grouped{CHUNKS[-1][0]}", align_bytes=64)
        rest_scales = keep.tile([P, 2 * rest_width], U8, name="rest_scales", align_bytes=64)
        rest_q = (rest_codes, rest_scales)
        for t0, t1 in ((1, 2), (2, PACK)):
            for base, grouped in ((0, w2_grouped), (rest_width, w3_grouped)):
                quantize(rest_q, base + (t0 - 1) * P, base + (t1 - 1) * P, grouped[:, t0 * PACK * P : t1 * PACK * P])
        for t in range(1, PACK):
            product(h_banks[t][:], rest_q, (t - 1) * P, hidden_q, 0, S, True, False)
            product(h_banks[t][:], rest_q, rest_width + (t - 1) * P, hidden_q, S, 2 * S, False, True)
            nc.scalar.activation(windows[t][:, :S], h_banks[t][:], ACT.Copy, scale=0.75)
            nc.scalar.activation(neg_h[t][:], h_banks[t][:], ACT.Copy, scale=-1.0)

        out_rows = out.rearrange("(p t) n -> p t n", t=PACK)
        for t in range(PACK):
            partial = keep.tile([P, S], F32, name=f"partial{t}")
            result = keep.tile([P, S], F32, name=f"result{t}")
            for lo in (0, HALF):
                cols = slice(lo, lo + HALF)
                looked_up = windows[t][:].indirect(entries(list5, lo, lo + HALF))
                nc.vector.tensor_tensor(partial[:, cols], looked_up, neg_h[t][:, cols], ALU.add)
            for lo in (0, HALF):
                cols = slice(lo, lo + HALF)
                looked_up = windows[t][:].indirect(entries(list6, lo, lo + HALF))
                nc.vector.tensor_tensor(result[:, cols], looked_up, partial[:, cols], ALU.add)
                if t == PACK - 1:
                    nc.sync.dma_start(out_rows[:, t, cols], result[:, cols])
            if t < PACK - 1:
                nc.sync.dma_start(out_rows[:, t, :], result[:])
